import numpy as np
import ml_dtypes

BF16 = ml_dtypes.bfloat16


def bf(x):
    return np.asarray(x, np.float32).astype(BF16)


def f32(x):
    return np.asarray(x, np.float32)


def f64(x):
    return np.asarray(x).astype(np.float64)


def striped(idx):
    return np.concatenate([l.reshape(-1, 16).T for l in idx])


def rows(idx, k):
    return np.tile(np.repeat(idx, 16, axis=0), (k // (16 * 8), 1))


def look(tab, idx):
    return np.take_along_axis(f64(tab), rows(idx, len(tab)), axis=1)


K, S, V, N = 128, 2048, 1024, 1024


def setup_inputs():
    return {"tab": f32(np.random.standard_normal((2, K, S))), "y": f32(np.random.standard_normal((K, V))), "offs": striped(np.stack([np.random.permutation(S)[:N] for _ in range(8)]))}


def reference(tab, y, offs):
    idx = np.stack([g.T.reshape(-1) for g in np.split(offs, 8)])
    x = (look(tab[0], idx) - f64(y)) * (1.0 / (1.0 + np.exp(-look(tab[1], idx))))
    return x

@@ -1,0 +1,40 @@
+import concourse.mybir as mybir
+
+F32 = mybir.dt.float32
+U16 = mybir.dt.uint16
+SUBTRACT = mybir.AluOpType.subtract
+MULT = mybir.AluOpType.mult
+SIGMOID = mybir.ActivationFunctionType.Sigmoid
+
+GROUP = 16
+PIECE = 512
+
+
+def tile_lookup_vg_subsig_out_kernel(tc, tab, y, offs, out):
+    nc = tc.nc
+    rows, places = tab.shape[1], tab.shape[2]
+    entries = y.shape[1]
+    pieces = entries // PIECE
+
+    with tc.tile_pool(name="held", bufs=1) as held:
+        offsets = held.tile([rows, entries // GROUP], U16, name="offsets")
+        values = held.tile([rows, places], F32, name="values")
+        gates = held.tile([rows, places], F32, name="gates")
+        streams = [held.tile([rows, PIECE], F32, name=f"stream{p}") for p in range(pieces)]
+
+        nc.sync.dma_start(offsets[:], offs)
+        nc.sync.dma_start(values[:], tab[0])
+        nc.sync.dma_start(streams[0][:], y[:, 0:PIECE])
+        nc.sync.dma_start(gates[:], tab[1])
+        for p in range(1, pieces):
+            nc.sync.dma_start(streams[p][:], y[:, p * PIECE : (p + 1) * PIECE])
+
+        for p in range(pieces):
+            listed = offsets[:, p * PIECE // GROUP : (p + 1) * PIECE // GROUP]
+            diff = held.tile([rows, PIECE], F32, name=f"diff{p}")
+            gate = held.tile([rows, PIECE], F32, name=f"gate{p}")
+            result = held.tile([rows, PIECE], F32, name=f"result{p}")
+            nc.vector.tensor_tensor(diff[:], values[:].indirect(listed), streams[p][:], SUBTRACT)
+            nc.scalar.activation(gate[:], gates[:].indirect(listed), SIGMOID)
+            nc.vector.tensor_tensor(result[:], diff[:], gate[:], MULT)
+            nc.sync.dma_start(out[:, p * PIECE : (p + 1) * PIECE], result[:])

@@ -8,6 +8,7 @@ SIGMOID = mybir.ActivationFunctionType.Sigmoid
 
 GROUP = 16
 PIECE = 512
+WARM = 8
 
 
 def tile_lookup_vg_subsig_out_kernel(tc, tab, y, offs, out):
@@ -21,6 +22,9 @@ def tile_lookup_vg_subsig_out_kernel(tc, tab, y, offs, out):
         values = held.tile([rows, places], F32, name="values")
         gates = held.tile([rows, places], F32, name="gates")
         streams = [held.tile([rows, PIECE], F32, name=f"stream{p}") for p in range(pieces)]
+        diffs = [held.tile([rows, PIECE], F32, name=f"diff{p}") for p in range(pieces)]
+        sigmoids = [held.tile([rows, PIECE], F32, name=f"sigmoid{p}") for p in range(pieces)]
+        results = [held.tile([rows, PIECE], F32, name=f"result{p}") for p in range(pieces)]
 
         nc.sync.dma_start(offsets[:], offs)
         nc.sync.dma_start(values[:], tab[0])
@@ -29,12 +33,15 @@ def tile_lookup_vg_subsig_out_kernel(tc, tab, y, offs, out):
         for p in range(1, pieces):
             nc.sync.dma_start(streams[p][:], y[:, p * PIECE : (p + 1) * PIECE])
 
+        warm_in = held.tile([rows, WARM], F32, name="warm_in")
+        warm_out = held.tile([rows, WARM], F32, name="warm_out")
+        nc.vector.memset(warm_in[:], 0.0)
+        nc.scalar.activation(warm_out[:], warm_in[:], SIGMOID)
+
         for p in range(pieces):
             listed = offsets[:, p * PIECE // GROUP : (p + 1) * PIECE // GROUP]
-            diff = held.tile([rows, PIECE], F32, name=f"diff{p}")
-            gate = held.tile([rows, PIECE], F32, name=f"gate{p}")
-            result = held.tile([rows, PIECE], F32, name=f"result{p}")
-            nc.vector.tensor_tensor(diff[:], values[:].indirect(listed), streams[p][:], SUBTRACT)
-            nc.scalar.activation(gate[:], gates[:].indirect(listed), SIGMOID)
-            nc.vector.tensor_tensor(result[:], diff[:], gate[:], MULT)
-            nc.sync.dma_start(out[:, p * PIECE : (p + 1) * PIECE], result[:])
+            nc.vector.tensor_tensor(diffs[p][:], values[:].indirect(listed), streams[p][:], SUBTRACT)
+            nc.scalar.activation(sigmoids[p][:], gates[:].indirect(listed), SIGMOID)
+        for p in range(pieces):
+            nc.vector.tensor_tensor(results[p][:], diffs[p][:], sigmoids[p][:], MULT)
+            nc.sync.dma_start(out[:, p * PIECE : (p + 1) * PIECE], results[p][:])

@@ -28,7 +28,7 @@ def tile_lookup_vg_subsig_out_kernel(tc, tab, y, offs, out):
 
         nc.sync.dma_start(offsets[:], offs)
         nc.sync.dma_start(values[:], tab[0])
-        nc.sync.dma_start(streams[0][:], y[:, 0:PIECE])
+        nc.scalar.dma_start(streams[0][:], y[:, 0:PIECE])
         nc.sync.dma_start(gates[:], tab[1])
         for p in range(1, pieces):
             nc.sync.dma_start(streams[p][:], y[:, p * PIECE : (p + 1) * PIECE])

import concourse.mybir as mybir

F32 = mybir.dt.float32
U16 = mybir.dt.uint16
SUBTRACT = mybir.AluOpType.subtract
MULT = mybir.AluOpType.mult
SIGMOID = mybir.ActivationFunctionType.Sigmoid

GROUP = 16
PIECE = 512
WARM = 8


def tile_lookup_vg_subsig_out_kernel(tc, tab, y, offs, out):
    nc = tc.nc
    rows, places = tab.shape[1], tab.shape[2]
    entries = y.shape[1]
    pieces = entries // PIECE

    with tc.tile_pool(name="held", bufs=1) as held:
        offsets = held.tile([rows, entries // GROUP], U16, name="offsets")
        values = held.tile([rows, places], F32, name="values")
        gates = held.tile([rows, places], F32, name="gates")
        streams = [held.tile([rows, PIECE], F32, name=f"stream{p}") for p in range(pieces)]
        diffs = [held.tile([rows, PIECE], F32, name=f"diff{p}") for p in range(pieces)]
        sigmoids = [held.tile([rows, PIECE], F32, name=f"sigmoid{p}") for p in range(pieces)]
        results = [held.tile([rows, PIECE], F32, name=f"result{p}") for p in range(pieces)]

        nc.sync.dma_start(offsets[:], offs)
        nc.sync.dma_start(values[:], tab[0])
        nc.scalar.dma_start(streams[0][:], y[:, 0:PIECE])
        nc.sync.dma_start(gates[:], tab[1])
        for p in range(1, pieces):
            nc.sync.dma_start(streams[p][:], y[:, p * PIECE : (p + 1) * PIECE])

        warm_in = held.tile([rows, WARM], F32, name="warm_in")
        warm_out = held.tile([rows, WARM], F32, name="warm_out")
        nc.vector.memset(warm_in[:], 0.0)
        nc.scalar.activation(warm_out[:], warm_in[:], SIGMOID)

        for p in range(pieces):
            listed = offsets[:, p * PIECE // GROUP : (p + 1) * PIECE // GROUP]
            nc.vector.tensor_tensor(diffs[p][:], values[:].indirect(listed), streams[p][:], SUBTRACT)
            nc.scalar.activation(sigmoids[p][:], gates[:].indirect(listed), SIGMOID)
        for p in range(pieces):
            nc.vector.tensor_tensor(results[p][:], diffs[p][:], sigmoids[p][:], MULT)
            nc.sync.dma_start(out[:, p * PIECE : (p + 1) * PIECE], results[p][:])
